import numpy as np
import ml_dtypes


def mxq(x, axis, fmt="e4m3"):
    dtype, down = {"e4m3": (ml_dtypes.float8_e4m3fn, 7), "e5m2": (ml_dtypes.float8_e5m2, 14)}[fmt]
    v = np.moveaxis(np.asarray(x, np.float32).astype(ml_dtypes.bfloat16).astype(np.float64), axis, -1)
    blocks = v.reshape(v.shape[:-1] + (-1, 32))
    amax = np.abs(blocks).max(-1, keepdims=True)
    byte = np.maximum(np.where(amax > 0, np.frexp(amax)[1] - 1 + 127, 0) - down, 1)
    scale = np.exp2(byte - 127.0)
    codes = (blocks / scale).astype(np.float32).astype(dtype).astype(np.float64)
    return np.moveaxis((codes * scale).reshape(v.shape), -1, axis)


WIDE = False


def mx_kscale(k):
    if not WIDE:
        return np.ones(k)
    levels = np.array([10, -10, 5, -5, 0])
    if k % 512:
        return np.exp2(np.random.permutation(np.resize(levels, k // 32))).repeat(32)
    a = np.empty((k // 512, 16))
    for p in range(k // 512):
        a[p, :8] = np.random.permutation(np.resize(levels, 8))
        for g in range(8):
            far = levels[np.abs(levels - a[p, g]) >= 10]
            a[p, g + 8] = far[np.random.randint(len(far))]
    return np.exp2(a.ravel()).repeat(32)


def f64(x):
    return np.asarray(x).astype(np.float64)


def striped(idx):
    return np.tile(idx.reshape(-1, 16).T, (8, 1)).astype(np.uint16)


def unstriped(offs):
    return offs[:16].T.reshape(-1).astype(np.int64)


E2M1 = np.array([0.0, 0.5, 1.0, 1.5, 2.0, 3.0, 4.0, 6.0, -0.0, -0.5, -1.0, -1.5, -2.0, -3.0, -4.0, -6.0])


def pack_weight(w, fmt):
    k, n = w.shape
    w = f64(np.asarray(w, np.float32).astype(ml_dtypes.bfloat16)).reshape(k // 32, 32, n)
    amax = np.abs(w).max(1)
    if fmt == "e4m3":
        byte = np.frexp(amax)[1] - 1 + 127 - 7
    else:
        mant, ex = np.frexp(amax / 6.0)
        byte = np.where(mant > 0.5, ex, ex - 1) + 127
    byte = np.clip(np.where(amax > 0, byte, 1), 1, 254)
    scaled = (w * np.exp2(127.0 - byte)[:, None, :]).reshape(k, n).astype(np.float32)
    by_word = np.ascontiguousarray(scaled.reshape(k // 512, 128, 4, n).transpose(0, 1, 3, 2))
    if fmt == "e4m3":
        words = by_word.astype(ml_dtypes.float8_e4m3fn).view(np.uint8)
    else:
        c = by_word.astype(ml_dtypes.float4_e2m1fn).view(np.uint8) & 0xF
        words = (c[..., 0::2] | (c[..., 1::2] << 4)).reshape(k // 512, 128, 2 * n)
    return np.ascontiguousarray(words), np.ascontiguousarray(byte.astype(np.uint8).reshape(k // 512, 16, n))


def unpack_weight(words, scales, fmt):
    g, _, n = scales.shape
    words = np.ascontiguousarray(words).reshape(g, 128, n, -1)
    if fmt == "e4m3":
        vals = words.view(ml_dtypes.float8_e4m3fn).astype(np.float64)
    else:
        nib = np.empty((g, 128, n, 4), np.uint8)
        nib[..., 0::2] = words & 0xF
        nib[..., 1::2] = words >> 4
        vals = E2M1[nib]
    vals = vals * np.repeat(np.exp2(scales.astype(np.float64) - 127.0), 8, axis=1)[..., None]
    return vals.transpose(0, 1, 3, 2).reshape(g * 512, n)


def gelu(v):
    return 0.5 * v * (1.0 + np.tanh(np.sqrt(2.0 / np.pi) * (v + 0.044715 * v**3)))


def bf(x):
    return np.asarray(x, np.float32).astype(ml_dtypes.bfloat16)


def planes(Y):
    n, m = Y.shape
    b = f64(bf(Y)).reshape(n // 32, 32, m)
    amax = np.abs(b).max(1)
    byte = np.clip(np.where(amax > 0, np.frexp(amax)[1] - 1 + 127 - 7, 1), 1, 254)
    codes = (b * np.exp2(127.0 - byte)[:, None, :]).reshape(n, m).astype(np.float32).astype(ml_dtypes.float8_e4m3fn).view(np.uint8)
    words = codes.reshape(n // 512, 128, 4, m).transpose(0, 1, 3, 2)
    return np.ascontiguousarray(words), np.ascontiguousarray(byte.astype(np.uint8).reshape(n // 512, 16, m))


K, T, S, P, H, N = 1536, 4096, 1024, 512, 512, 1024

def setup_inputs():
    n = np.random.standard_normal
    s = mx_kscale(K)[:, None]
    u = mx_kscale(H)[:, None]
    u2 = mx_kscale(N)[:, None]
    lam = np.exp(0.8 * n(N))
    tab_words, tab_scales = pack_weight(n((K, T)) * s, "e4m3")
    w2_words, w2_scales = pack_weight(1.2 * n((H, N)) / np.sqrt(H) / u, "e2m1")
    return {
        "tab_words": tab_words, "tab_scales": tab_scales,
        "offs": striped(np.random.permutation(T)[:S]),
        "pos1": striped(np.random.permutation(S)[:P]),
        "pos2": striped(np.random.permutation(S)[:P]),
        "w1": (0.85 * n((K, H)) / np.sqrt(K) / s).astype(np.float32),
        "slope": np.random.uniform(1, 3, H).astype(np.float32),
        "share": np.random.uniform(0.1, 0.5, H).astype(np.float32),
        "posture": (3.0 * n((H, P)) * u).astype(np.float32),
        "w2_words": w2_words, "w2_scales": w2_scales,
        "gain": (np.random.uniform(0.5, 2.0, N) * u2[:, 0]).astype(np.float32),
        "w3": (1.2 * n((N, N)) / np.sqrt(N) / u2 * lam[None, :]).astype(np.float32),
        "skip": (np.random.uniform(0.4, 1.2, N) * lam).astype(np.float32),
    }

def reference(tab_words, tab_scales, offs, pos1, pos2, w1, slope, share, posture,
              w2_words, w2_scales, gain, w3, skip):
    v = unpack_weight(tab_words, tab_scales, "e4m3")[:, unstriped(offs)]
    h = mxq(f64(w1), 0, "e4m3").T @ v
    top = h.max(axis=1)
    a = 1.0 / (1.0 + np.exp(-f64(slope)[:, None] * (h[:, unstriped(pos1)] - f64(share)[:, None] * top[:, None])))
    c = h[:, unstriped(pos2)]
    f = mxq(a * c * f64(posture), 0, "e4m3")
    w2 = unpack_weight(w2_words, w2_scales, "e2m1")
    d = w2.T @ f
    t = mxq(f64(gain)[:, None] * np.tanh(d), 0, "e4m3")
    y = (mxq(f64(w3), 0, "e4m3").T @ t) + f64(skip)[:, None] * d
    words, scales = planes(y)
    return y, words, scales

@@ -1,0 +1,323 @@
+from contextlib import ExitStack
+
+import concourse.mybir as mybir
+
+K, T, S, J, H, N = 1536, 4096, 1024, 512, 512, 1024
+FLOPS = 2 * (K * H * S + H * N * J + N * N * J)
+
+F32 = mybir.dt.float32
+BF16 = mybir.dt.bfloat16
+I32 = mybir.dt.int32
+U32 = mybir.dt.uint32
+U16 = mybir.dt.uint16
+U8 = mybir.dt.uint8
+FP8X4 = mybir.dt.float8_e4m3fn_x4
+FP4X4 = mybir.dt.float4_e2m1fn_x4
+ALU = mybir.AluOpType
+ACT = mybir.ActivationFunctionType
+
+P = 128
+PACK = 4
+PASS = P * PACK
+BANK = 512
+HALF = J // 2
+LINE = 4
+
+
+def tile_list_posture_relief_features_kernel(
+    tc, tab_words, tab_scales, offs, pos1, pos2, w1, slope, share, posture,
+    w2_words, w2_scales, gain, w3, skip, out_0, out_1, out_2,
+):
+    nc = tc.nc
+    k_passes = K // PASS
+    n_groups = N // PASS
+
+    with ExitStack() as ctx:
+        lists = ctx.enter_context(tc.tile_pool(name="lists", bufs=1))
+        keep = ctx.enter_context(tc.tile_pool(name="keep", bufs=1))
+        psum = ctx.enter_context(tc.psum_pool(name="psum", bufs=1))
+
+        def sb(name, shape, dtype, over=None):
+            return keep.tile(shape, dtype, name=name, tag=over or name, align_bytes=64)
+
+        banks = [psum.tile([P, BANK], F32, name=f"bank{b}") for b in range(8)]
+
+        offs_sb = lists.tile([P, S // 16], U16, name="offs_sb")
+        pos1_sb = lists.tile([P, J // 16], U16, name="pos1_sb")
+        pos2_sb = lists.tile([P, J // 16], U16, name="pos2_sb")
+
+        tab_sb = [sb(f"tab{a}", [P, T], U32) for a in range(k_passes)]
+        tabs_sb = sb("tabs", [P, T], U8)
+        w2s_raw = sb("w2s_raw", [P, N], U8)
+        w2_raw = sb("w2_raw", [P, 2 * N], U8)
+        nc.vector.memset(tabs_sb[:].bitcast(I32), 0)
+        nc.vector.memset(w2s_raw[:].bitcast(I32), 0)
+        slope_sb = sb("slope_sb", [P, PACK], F32)
+        share_sb = sb("share_sb", [P, PACK], F32)
+        gain_sb = sb("gain_sb", [P, n_groups, PACK], F32)
+        skip_sb = sb("skip_sb", [P, n_groups, PACK], F32)
+        nc.gpsimd.dma_start(out=slope_sb[:], in_=slope.rearrange("(p t) -> p t", t=PACK))
+        nc.gpsimd.dma_start(out=share_sb[:], in_=share.rearrange("(p t) -> p t", t=PACK))
+        nc.gpsimd.dma_start(out=gain_sb[:], in_=gain.rearrange("(g p t) -> p g t", p=P, t=PACK))
+        nc.gpsimd.dma_start(out=skip_sb[:], in_=skip.rearrange("(g p t) -> p g t", p=P, t=PACK))
+
+        def load_tab(a):
+            nc.sync.dma_start(
+                out=tab_sb[a][:].bitcast(I32),
+                in_=tab_words[a].rearrange("p t i -> p (t i)").bitcast(I32),
+            )
+
+        def load_rows(name, w, a, c0, c1):
+            raw = sb(name, [P, PACK, c1 - c0], F32)
+            nc.sync.dma_start(
+                out=raw[:], in_=w[a * PASS : (a + 1) * PASS, c0:c1].rearrange("(p j) c -> p j c", j=PACK)
+            )
+            return raw
+
+        load_tab(0)
+        for q in range(4):
+            nc.sync.dma_start(
+                out=tabs_sb[32 * q : 32 * q + 4 * k_passes, :].bitcast(I32),
+                in_=tab_scales[:, 4 * q : 4 * q + 4, :].bitcast(I32),
+            )
+        nc.sync.dma_start(offs_sb[:], offs)
+        w1_raw = [load_rows("w1_raw0", w1, 0, 0, H)]
+        load_tab(1)
+        for q in range(4):
+            nc.sync.dma_start(
+                out=w2s_raw[32 * q : 32 * q + 4, :].bitcast(I32),
+                in_=w2_scales[0, 4 * q : 4 * q + 4, :].bitcast(I32),
+            )
+        nc.sync.dma_start(out=w2_raw[:].bitcast(I32), in_=w2_words[0].bitcast(I32))
+        nc.sync.dma_start(pos1_sb[:], pos1)
+        nc.sync.dma_start(pos2_sb[:], pos2)
+        w1_raw.append(load_rows("w1_raw1", w1, 1, 0, H))
+        load_tab(2)
+        w1_last = [load_rows(f"w1_last{c}", w1, 2, c * (H // 2), (c + 1) * (H // 2)) for c in range(2)]
+        w3_raw = {}
+        w3_raw[0, 0] = load_rows("w3_raw00", w3, 0, 0, PASS)
+        posture_sb = sb("posture_sb", [P, PACK, J], F32)
+        nc.sync.dma_start(out=posture_sb[:], in_=posture.rearrange("(p t) j -> p t j", t=PACK))
+        w3_raw[1, 0] = load_rows("w3_raw10", w3, 1, 0, PASS)
+        w3_raw[0, 1] = load_rows("w3_raw01", w3, 0, PASS, N)
+        w3_raw[1, 1] = load_rows("w3_raw11", w3, 1, PASS, N)
+
+        def deal(copy, grouped, raw, m0, m1, raw_m0=0):
+            copy(
+                grouped[:, :, m0:m1, :].rearrange("p t m j -> p m j t"),
+                raw[:].rearrange("p j (m t) -> p m j t", t=PACK)[:, m0 - raw_m0 : m1 - raw_m0],
+            )
+
+        def quantize(codes, scales, values):
+            nc.vector.quantize_mx(out=codes.bitcast(FP8X4), scales=scales, in_=values)
+
+        nss = sb("nss", [P, PACK], F32)
+        nc.vector.scalar_tensor_tensor(nss[:], slope_sb[:], -1.0, share_sb[:], ALU.mult, ALU.mult)
+
+        w2_sb = sb("w2_sb", [P, 2 * N], U8)
+        w2s_sb = sb("w2s_sb", [P, N], U8)
+        nc.vector.tensor_copy(
+            w2_sb[:].rearrange("p (g t m e) -> p g t m e", g=n_groups, t=PACK, e=2),
+            w2_raw[:].rearrange("p (g m t e) -> p g t m e", g=n_groups, t=PACK, e=2),
+        )
+        nc.vector.tensor_copy(
+            w2s_sb[:].rearrange("p (g t m) -> p g t m", g=n_groups, t=PACK),
+            w2s_raw[:].rearrange("p (g m t) -> p g t m", g=n_groups, t=PACK),
+        )
+
+        vs_sb = sb("vs_sb", [P, S], U8)
+        nc.vector.tensor_copy(vs_sb[:], tabs_sb[:].indirect(offs_sb[:]))
+
+        v_sb = [sb(f"v{a}", [P, S], U32) for a in range(k_passes)]
+        w1_bf = [sb(f"w1_bf{a}", [P, PACK, P, PACK], BF16) for a in range(k_passes)]
+        w1_codes = [sb(f"w1_codes{a}", [P, H], U32) for a in range(k_passes)]
+        w1_scales = [sb(f"w1_scales{a}", [P, H], U8) for a in range(k_passes)]
+
+        def mm1(a, t, c):
+            nc.tensor.matmul_mx(
+                out=banks[2 * t + c][:],
+                lhsT=w1_codes[a][:, t * P : (t + 1) * P].bitcast(FP8X4),
+                lhsT_scale=w1_scales[a][:, t * P : (t + 1) * P],
+                rhs=v_sb[a][:, c * BANK : (c + 1) * BANK].bitcast(FP8X4),
+                rhs_scale=vs_sb[4 * a : P, c * BANK : (c + 1) * BANK],
+                start=(a == 0),
+                stop=(a == k_passes - 1),
+            )
+
+        for a in range(k_passes):
+            nc.vector.tensor_copy(v_sb[a][:], tab_sb[a][:].indirect(offs_sb[:]))
+            if a < k_passes - 1:
+                deal(nc.scalar.copy, w1_bf[a], w1_raw[a], 0, P)
+                quantize(w1_codes[a][:], w1_scales[a][:], w1_bf[a][:].rearrange("p t m j -> p (t m j)"))
+            else:
+                for c in range(2):
+                    m0 = c * 64
+                    deal(nc.vector.tensor_copy, w1_bf[a], w1_last[c], m0, m0 + 42, m0)
+                    deal(nc.scalar.copy, w1_bf[a], w1_last[c], m0 + 42, m0 + 64, m0)
+                    for t in range(PACK):
+                        cols = slice(t * P + m0, t * P + m0 + 64)
+                        quantize(
+                            w1_codes[a][:, cols], w1_scales[a][:, cols],
+                            w1_bf[a][:, t, m0 : m0 + 64, :].rearrange("p m j -> p (m j)"),
+                        )
+            for t in range(PACK):
+                for c in range(2):
+                    mm1(a, t, c)
+
+        h_sb = [sb(f"h{t}", [P, S], F32) for t in range(PACK)]
+        tops = sb("tops", [P, PACK, 2], F32)
+        bias = sb("bias", [P, PACK], F32)
+        for t in range(PACK):
+            for c in range(2):
+                nc.vector.tensor_scalar(
+                    h_sb[t][:, c * BANK : (c + 1) * BANK], banks[2 * t + c][:], 1.0, None,
+                    ALU.mult, ALU.max, accum_out=tops[:, t, c : c + 1],
+                )
+            nc.gpsimd.tensor_scalar(
+                bias[:, t : t + 1], tops[:, t, 0:1], tops[:, t, 1:2], nss[:, t : t + 1], ALU.max, ALU.mult
+            )
+
+        th = {}
+        sd = {}
+
+        def stage2(c):
+            cols16 = slice(c * HALF // 16, (c + 1) * HALF // 16)
+            a_sb = sb(f"a{c}", [P, PACK, HALF], F32)
+            c_sb = sb(f"c{c}", [P, PACK, HALF], F32)
+            for t in range(PACK):
+                nc.scalar.activation(
+                    out=a_sb[:, t, :], in_=h_sb[t][:].indirect(pos1_sb[:, cols16]), func=ACT.Sigmoid,
+                    bias=bias[:, t : t + 1], scale=slope_sb[:, t : t + 1],
+                )
+                nc.vector.tensor_tensor(
+                    c_sb[:, t, :], h_sb[t][:].indirect(pos2_sb[:, cols16]),
+                    posture_sb[:, t, c * HALF : (c + 1) * HALF], ALU.mult,
+                )
+            f_bf = sb(f"f_bf{c}", [P, HALF, PACK], BF16)
+            nc.vector.tensor_tensor(
+                f_bf[:].rearrange("p (x i) t -> p x t i", i=LINE),
+                a_sb[:].rearrange("p t (x i) -> p x t i", i=LINE),
+                c_sb[:].rearrange("p t (x i) -> p x t i", i=LINE),
+                ALU.mult,
+            )
+            f_codes = sb(f"f_codes{c}", [P, HALF], U32)
+            f_scales = sb(f"f_scales{c}", [P, HALF], U8)
+            quantize(f_codes[:], f_scales[:], f_bf[:].rearrange("p j t -> p (j t)"))
+            for g in range(n_groups):
+                for t in range(PACK):
+                    s = PACK * g + t
+                    nc.tensor.matmul_mx(
+                        out=banks[4 * c + s // 2][:, (s % 2) * HALF : (s % 2 + 1) * HALF],
+                        lhsT=w2_sb[:, 2 * s * P : 2 * (s + 1) * P].bitcast(FP4X4),
+                        lhsT_scale=w2s_sb[:, s * P : (s + 1) * P],
+                        rhs=f_codes[:].bitcast(FP8X4),
+                        rhs_scale=f_scales[:],
+                        start=True,
+                        stop=True,
+                    )
+
+        def tanh_d(c):
+            for g in range(n_groups):
+                th[c, g] = sb(f"th{c}{g}", [P, 2, HALF, 2], F32, ["w1_raw0", "w1_raw1", "w1_last0", "w1_last1"][2 * c + g])
+                for u in range(2):
+                    nc.scalar.activation(
+                        out=th[c, g][:, u], in_=banks[4 * c + 2 * g + u][:].rearrange("p (e j) -> p j e", e=2),
+                        func=ACT.Tanh,
+                    )
+
+        def skip_d(c):
+            for g in range(n_groups):
+                sd[c, g] = sb(f"sd{c}{g}", [P, PACK, HALF], F32, ["w1_bf0", "w1_bf1", "w1_bf2", "posture_sb"][2 * c + g])
+                for t in range(PACK):
+                    nc.scalar.activation(
+                        out=sd[c, g][:, t, :],
+                        in_=banks[4 * c + 2 * g + t // 2][:, (t % 2) * HALF : (t % 2 + 1) * HALF],
+                        func=ACT.Copy, scale=skip_sb[:, g, t : t + 1],
+                    )
+
+        w3_codes = {}
+        w3_scales = {}
+
+        def prep_w3(g, o):
+            bf = sb(f"w3_bf{g}{o}", [P, PACK, P, PACK], BF16)
+            for c in range(2):
+                deal(nc.scalar.copy, bf, w3_raw[g, o], c * 64, (c + 1) * 64)
+            w3_codes[g, o] = sb(f"w3_codes{g}{o}", [P, PASS], U32)
+            w3_scales[g, o] = sb(f"w3_scales{g}{o}", [P, PASS], U8)
+            quantize(w3_codes[g, o][:], w3_scales[g, o][:], bf[:].rearrange("p t m j -> p (t m j)"))
+
+        t_codes = {}
+        t_scales = {}
+
+        def quant_t(c):
+            for g in range(n_groups):
+                t_bf = sb(f"t_bf{c}{g}", [P, HALF, PACK], BF16, f"w3_raw{g}0" if c == 1 else None)
+                nc.vector.tensor_tensor(
+                    t_bf[:].rearrange("p j (u e) -> p j u e", e=2),
+                    th[c, g][:].rearrange("p u j e -> p j u e"),
+                    gain_sb[:, g, :].rearrange("p (u e) -> p u e", e=2).unsqueeze(1).to_broadcast([P, HALF, 2, 2]),
+                    ALU.mult,
+                )
+                t_codes[c, g] = sb(f"t_codes{c}{g}", [P, HALF], U32)
+                t_scales[c, g] = sb(f"t_scales{c}{g}", [P, HALF], U8)
+                quantize(t_codes[c, g][:], t_scales[c, g][:], t_bf[:].rearrange("p j t -> p (j t)"))
+
+        y_scales = sb("y_scales", [P, n_groups, J], U8)
+
+        def stage3(c):
+            cols = slice(c * HALF, (c + 1) * HALF)
+            for o in range(n_groups):
+                for t in range(PACK):
+                    for g in range(n_groups):
+                        nc.tensor.matmul_mx(
+                            out=banks[4 * c + 2 * o + t // 2][:, (t % 2) * HALF : (t % 2 + 1) * HALF],
+                            lhsT=w3_codes[g, o][:, t * P : (t + 1) * P].bitcast(FP8X4),
+                            lhsT_scale=w3_scales[g, o][:, t * P : (t + 1) * P],
+                            rhs=t_codes[c, g][:].bitcast(FP8X4),
+                            rhs_scale=t_scales[c, g][:],
+                            start=(g == 0),
+                            stop=(g == n_groups - 1),
+                        )
+            for o in range(n_groups):
+                y_sb = sb(f"y{c}{o}", [P, PACK, HALF], F32, f"{'ac'[o]}{c}")
+                for u in range(2):
+                    nc.vector.tensor_tensor(
+                        y_sb[:, 2 * u : 2 * u + 2, :].rearrange("p t j -> p (t j)"),
+                        banks[4 * c + 2 * o + u][:],
+                        sd[c, o][:, 2 * u : 2 * u + 2, :].rearrange("p t j -> p (t j)"),
+                        ALU.add,
+                    )
+                nc.sync.dma_start(
+                    out=out_0[o * PASS : (o + 1) * PASS, cols].rearrange("(p t) j -> p t j", t=PACK), in_=y_sb[:]
+                )
+                y_bf = sb(f"y_bf{c}{o}", [P, HALF, PACK], BF16, f"w3_bf{c}{o}")
+                nc.scalar.copy(
+                    y_bf[:].rearrange("p (x i) t -> p x t i", i=LINE),
+                    y_sb[:].rearrange("p t (x i) -> p x t i", i=LINE),
+                )
+                y_codes = sb(f"y_codes{c}{o}", [P, HALF], U32)
+                quantize(y_codes[:], y_scales[:, o, cols], y_bf[:].rearrange("p j t -> p (j t)"))
+                nc.sync.dma_start(
+                    out=out_1[o].rearrange("p j t -> p (j t)")[:, PACK * c * HALF : PACK * (c + 1) * HALF].bitcast(I32),
+                    in_=y_codes[:].bitcast(I32),
+                )
+
+        stage2(0)
+        stage2(1)
+        tanh_d(0)
+        prep_w3(0, 0)
+        prep_w3(1, 0)
+        prep_w3(0, 1)
+        prep_w3(1, 1)
+        quant_t(0)
+        tanh_d(1)
+        skip_d(0)
+        quant_t(1)
+        skip_d(1)
+        stage3(0)
+        stage3(1)
+        for q in range(4):
+            nc.sync.dma_start(
+                out=out_2[:, 4 * q : 4 * q + 4, :].rearrange("g r j -> r g j").bitcast(I32),
+                in_=y_scales[32 * q : 32 * q + 4].bitcast(I32),
+            )

@@ -50,16 +50,17 @@ def tile_list_posture_relief_features_kernel(
         tabs_sb = sb("tabs", [P, T], U8)
         w2s_raw = sb("w2s_raw", [P, N], U8)
         w2_raw = sb("w2_raw", [P, 2 * N], U8)
-        nc.vector.memset(tabs_sb[:].bitcast(I32), 0)
+        nc.gpsimd.memset(tabs_sb[:].bitcast(I32), 0)
         nc.vector.memset(w2s_raw[:].bitcast(I32), 0)
+        for q in range(4):
+            nc.gpsimd.dma_start(
+                out=tabs_sb[32 * q : 32 * q + 4 * k_passes, :].bitcast(I32),
+                in_=tab_scales[:, 4 * q : 4 * q + 4, :].bitcast(I32),
+            )
         slope_sb = sb("slope_sb", [P, PACK], F32)
         share_sb = sb("share_sb", [P, PACK], F32)
         gain_sb = sb("gain_sb", [P, n_groups, PACK], F32)
         skip_sb = sb("skip_sb", [P, n_groups, PACK], F32)
-        nc.gpsimd.dma_start(out=slope_sb[:], in_=slope.rearrange("(p t) -> p t", t=PACK))
-        nc.gpsimd.dma_start(out=share_sb[:], in_=share.rearrange("(p t) -> p t", t=PACK))
-        nc.gpsimd.dma_start(out=gain_sb[:], in_=gain.rearrange("(g p t) -> p g t", p=P, t=PACK))
-        nc.gpsimd.dma_start(out=skip_sb[:], in_=skip.rearrange("(g p t) -> p g t", p=P, t=PACK))
 
         def load_tab(a):
             nc.sync.dma_start(
@@ -74,21 +75,18 @@ def tile_list_posture_relief_features_kernel(
             )
             return raw
 
-        load_tab(0)
-        for q in range(4):
-            nc.sync.dma_start(
-                out=tabs_sb[32 * q : 32 * q + 4 * k_passes, :].bitcast(I32),
-                in_=tab_scales[:, 4 * q : 4 * q + 4, :].bitcast(I32),
-            )
-        nc.sync.dma_start(offs_sb[:], offs)
         w1_raw = [load_rows("w1_raw0", w1, 0, 0, H)]
-        load_tab(1)
+        load_tab(0)
+        nc.sync.dma_start(offs_sb[:], offs)
         for q in range(4):
             nc.sync.dma_start(
                 out=w2s_raw[32 * q : 32 * q + 4, :].bitcast(I32),
                 in_=w2_scales[0, 4 * q : 4 * q + 4, :].bitcast(I32),
             )
+        load_tab(1)
+        nc.sync.dma_start(out=slope_sb[:], in_=slope.rearrange("(p t) -> p t", t=PACK))
         nc.sync.dma_start(out=w2_raw[:].bitcast(I32), in_=w2_words[0].bitcast(I32))
+        nc.sync.dma_start(out=share_sb[:], in_=share.rearrange("(p t) -> p t", t=PACK))
         nc.sync.dma_start(pos1_sb[:], pos1)
         nc.sync.dma_start(pos2_sb[:], pos2)
         w1_raw.append(load_rows("w1_raw1", w1, 1, 0, H))
@@ -96,16 +94,26 @@ def tile_list_posture_relief_features_kernel(
         w1_last = [load_rows(f"w1_last{c}", w1, 2, c * (H // 2), (c + 1) * (H // 2)) for c in range(2)]
         w3_raw = {}
         w3_raw[0, 0] = load_rows("w3_raw00", w3, 0, 0, PASS)
-        posture_sb = sb("posture_sb", [P, PACK, J], F32)
-        nc.sync.dma_start(out=posture_sb[:], in_=posture.rearrange("(p t) j -> p t j", t=PACK))
+        posture_sb = [sb(f"posture{c}", [P, PACK, HALF], F32) for c in range(2)]
+
+        def load_posture(c):
+            nc.sync.dma_start(
+                out=posture_sb[c][:],
+                in_=posture[:, c * HALF : (c + 1) * HALF].rearrange("(p t) j -> p t j", t=PACK),
+            )
+
+        load_posture(0)
         w3_raw[1, 0] = load_rows("w3_raw10", w3, 1, 0, PASS)
+        load_posture(1)
+        nc.sync.dma_start(out=gain_sb[:], in_=gain.rearrange("(g p t) -> p g t", p=P, t=PACK))
+        nc.sync.dma_start(out=skip_sb[:], in_=skip.rearrange("(g p t) -> p g t", p=P, t=PACK))
         w3_raw[0, 1] = load_rows("w3_raw01", w3, 0, PASS, N)
         w3_raw[1, 1] = load_rows("w3_raw11", w3, 1, PASS, N)
 
         def deal(copy, grouped, raw, m0, m1, raw_m0=0):
             copy(
-                grouped[:, :, m0:m1, :].rearrange("p t m j -> p m j t"),
-                raw[:].rearrange("p j (m t) -> p m j t", t=PACK)[:, m0 - raw_m0 : m1 - raw_m0],
+                grouped[:, :, m0:m1, :].rearrange("p t m j -> p m t j"),
+                raw[:].rearrange("p j (m t) -> p m t j", t=PACK)[:, m0 - raw_m0 : m1 - raw_m0],
             )
 
         def quantize(codes, scales, values):
@@ -191,7 +199,7 @@ def tile_list_posture_relief_features_kernel(
                 )
                 nc.vector.tensor_tensor(
                     c_sb[:, t, :], h_sb[t][:].indirect(pos2_sb[:, cols16]),
-                    posture_sb[:, t, c * HALF : (c + 1) * HALF], ALU.mult,
+                    posture_sb[c][:, t, :], ALU.mult,
                 )
             f_bf = sb(f"f_bf{c}", [P, HALF, PACK], BF16)
             nc.vector.tensor_tensor(
@@ -227,7 +235,7 @@ def tile_list_posture_relief_features_kernel(
 
         def skip_d(c):
             for g in range(n_groups):
-                sd[c, g] = sb(f"sd{c}{g}", [P, PACK, HALF], F32, ["w1_bf0", "w1_bf1", "w1_bf2", "posture_sb"][2 * c + g])
+                sd[c, g] = sb(f"sd{c}{g}", [P, PACK, HALF], F32, ["w1_bf0", "w1_bf1", "w1_bf2", "posture0"][2 * c + g])
                 for t in range(PACK):
                     nc.scalar.activation(
                         out=sd[c, g][:, t, :],
@@ -264,43 +272,52 @@ def tile_list_posture_relief_features_kernel(
 
         y_scales = sb("y_scales", [P, n_groups, J], U8)
 
-        def stage3(c):
-            cols = slice(c * HALF, (c + 1) * HALF)
-            for o in range(n_groups):
-                for t in range(PACK):
-                    for g in range(n_groups):
-                        nc.tensor.matmul_mx(
-                            out=banks[4 * c + 2 * o + t // 2][:, (t % 2) * HALF : (t % 2 + 1) * HALF],
-                            lhsT=w3_codes[g, o][:, t * P : (t + 1) * P].bitcast(FP8X4),
-                            lhsT_scale=w3_scales[g, o][:, t * P : (t + 1) * P],
-                            rhs=t_codes[c, g][:].bitcast(FP8X4),
-                            rhs_scale=t_scales[c, g][:],
-                            start=(g == 0),
-                            stop=(g == n_groups - 1),
-                        )
-            for o in range(n_groups):
-                y_sb = sb(f"y{c}{o}", [P, PACK, HALF], F32, f"{'ac'[o]}{c}")
-                for u in range(2):
-                    nc.vector.tensor_tensor(
-                        y_sb[:, 2 * u : 2 * u + 2, :].rearrange("p t j -> p (t j)"),
-                        banks[4 * c + 2 * o + u][:],
-                        sd[c, o][:, 2 * u : 2 * u + 2, :].rearrange("p t j -> p (t j)"),
-                        ALU.add,
+        y_sb = {}
+        y_bf = {}
+
+        def mm3(c, o):
+            for t in range(PACK):
+                for g in range(n_groups):
+                    nc.tensor.matmul_mx(
+                        out=banks[4 * c + 2 * o + t // 2][:, (t % 2) * HALF : (t % 2 + 1) * HALF],
+                        lhsT=w3_codes[g, o][:, t * P : (t + 1) * P].bitcast(FP8X4),
+                        lhsT_scale=w3_scales[g, o][:, t * P : (t + 1) * P],
+                        rhs=t_codes[c, g][:].bitcast(FP8X4),
+                        rhs_scale=t_scales[c, g][:],
+                        start=(g == 0),
+                        stop=(g == n_groups - 1),
                     )
-                nc.sync.dma_start(
-                    out=out_0[o * PASS : (o + 1) * PASS, cols].rearrange("(p t) j -> p t j", t=PACK), in_=y_sb[:]
+
+        def add_y(c, o):
+            y_sb[c, o] = sb(f"y{c}{o}", [P, PACK, HALF], F32, f"{'ac'[o]}{c}")
+            for u in range(2):
+                nc.vector.tensor_tensor(
+                    y_sb[c, o][:, 2 * u : 2 * u + 2, :].rearrange("p t j -> p (t j)"),
+                    banks[4 * c + 2 * o + u][:],
+                    sd[c, o][:, 2 * u : 2 * u + 2, :].rearrange("p t j -> p (t j)"),
+                    ALU.add,
                 )
-                y_bf = sb(f"y_bf{c}{o}", [P, HALF, PACK], BF16, f"w3_bf{c}{o}")
-                nc.scalar.copy(
-                    y_bf[:].rearrange("p (x i) t -> p x t i", i=LINE),
-                    y_sb[:].rearrange("p t (x i) -> p x t i", i=LINE),
-                )
-                y_codes = sb(f"y_codes{c}{o}", [P, HALF], U32)
-                quantize(y_codes[:], y_scales[:, o, cols], y_bf[:].rearrange("p j t -> p (j t)"))
-                nc.sync.dma_start(
-                    out=out_1[o].rearrange("p j t -> p (j t)")[:, PACK * c * HALF : PACK * (c + 1) * HALF].bitcast(I32),
-                    in_=y_codes[:].bitcast(I32),
-                )
+            nc.sync.dma_start(
+                out=out_0[o * PASS : (o + 1) * PASS, c * HALF : (c + 1) * HALF].rearrange("(p t) j -> p t j", t=PACK),
+                in_=y_sb[c, o][:],
+            )
+
+        def round_y(c, o, copy):
+            y_bf[c, o] = sb(f"y_bf{c}{o}", [P, HALF, PACK], BF16, f"w3_bf{c}{o}")
+            copy(
+                y_bf[c, o][:].rearrange("p (x i) t -> p x t i", i=LINE),
+                y_sb[c, o][:].rearrange("p t (x i) -> p x t i", i=LINE),
+            )
+
+        def planes_y(c, o):
+            y_codes = sb(f"y_codes{c}{o}", [P, HALF], U32)
+            quantize(
+                y_codes[:], y_scales[:, o, c * HALF : (c + 1) * HALF], y_bf[c, o][:].rearrange("p j t -> p (j t)")
+            )
+            nc.sync.dma_start(
+                out=out_1[o].rearrange("p j t -> p (j t)")[:, PACK * c * HALF : PACK * (c + 1) * HALF].bitcast(I32),
+                in_=y_codes[:].bitcast(I32),
+            )
 
         stage2(0)
         stage2(1)
@@ -314,10 +331,24 @@ def tile_list_posture_relief_features_kernel(
         skip_d(0)
         quant_t(1)
         skip_d(1)
-        stage3(0)
-        stage3(1)
+        mm3(0, 0)
+        mm3(0, 1)
+        add_y(0, 0)
+        add_y(0, 1)
+        mm3(1, 0)
+        mm3(1, 1)
+        round_y(0, 0, nc.scalar.copy)
+        round_y(0, 1, nc.scalar.copy)
+        add_y(1, 0)
+        planes_y(0, 0)
+        add_y(1, 1)
+        round_y(1, 0, nc.scalar.copy)
+        planes_y(0, 1)
+        round_y(1, 1, nc.vector.tensor_copy)
+        planes_y(1, 0)
+        planes_y(1, 1)
         for q in range(4):
-            nc.sync.dma_start(
+            (nc.scalar, nc.sync)[q % 2].dma_start(
                 out=out_2[:, 4 * q : 4 * q + 4, :].rearrange("g r j -> r g j").bitcast(I32),
                 in_=y_scales[32 * q : 32 * q + 4].bitcast(I32),
             )

@@ -21,7 +21,7 @@ PACK = 4
 PASS = P * PACK
 BANK = 512
 HALF = J // 2
-LINE = 4
+LINE = 2
 
 
 def tile_list_posture_relief_features_kernel(
@@ -61,6 +61,10 @@ def tile_list_posture_relief_features_kernel(
         share_sb = sb("share_sb", [P, PACK], F32)
         gain_sb = sb("gain_sb", [P, n_groups, PACK], F32)
         skip_sb = sb("skip_sb", [P, n_groups, PACK], F32)
+        nc.gpsimd.dma_start(out=slope_sb[:], in_=slope.rearrange("(p t) -> p t", t=PACK))
+        nc.gpsimd.dma_start(out=share_sb[:], in_=share.rearrange("(p t) -> p t", t=PACK))
+        nc.gpsimd.dma_start(out=gain_sb[:], in_=gain.rearrange("(g p t) -> p g t", p=P, t=PACK))
+        nc.gpsimd.dma_start(out=skip_sb[:], in_=skip.rearrange("(g p t) -> p g t", p=P, t=PACK))
 
         def load_tab(a):
             nc.sync.dma_start(
@@ -75,7 +79,7 @@ def tile_list_posture_relief_features_kernel(
             )
             return raw
 
-        w1_raw = [load_rows("w1_raw0", w1, 0, 0, H)]
+        w1_raw = {0: load_rows("w1_raw0", w1, 0, 0, H)}
         load_tab(0)
         nc.sync.dma_start(offs_sb[:], offs)
         for q in range(4):
@@ -84,43 +88,36 @@ def tile_list_posture_relief_features_kernel(
                 in_=w2_scales[0, 4 * q : 4 * q + 4, :].bitcast(I32),
             )
         load_tab(1)
-        nc.sync.dma_start(out=slope_sb[:], in_=slope.rearrange("(p t) -> p t", t=PACK))
-        nc.sync.dma_start(out=w2_raw[:].bitcast(I32), in_=w2_words[0].bitcast(I32))
-        nc.sync.dma_start(out=share_sb[:], in_=share.rearrange("(p t) -> p t", t=PACK))
         nc.sync.dma_start(pos1_sb[:], pos1)
         nc.sync.dma_start(pos2_sb[:], pos2)
-        w1_raw.append(load_rows("w1_raw1", w1, 1, 0, H))
+        w1_raw[2] = load_rows("w1_raw2", w1, 2, 0, H)
+        w1_raw[1] = load_rows("w1_raw1", w1, 1, 0, H)
+        nc.sync.dma_start(out=w2_raw[:].bitcast(I32), in_=w2_words[0].bitcast(I32))
         load_tab(2)
-        w1_last = [load_rows(f"w1_last{c}", w1, 2, c * (H // 2), (c + 1) * (H // 2)) for c in range(2)]
         w3_raw = {}
         w3_raw[0, 0] = load_rows("w3_raw00", w3, 0, 0, PASS)
-        posture_sb = [sb(f"posture{c}", [P, PACK, HALF], F32) for c in range(2)]
-
-        def load_posture(c):
-            nc.sync.dma_start(
-                out=posture_sb[c][:],
-                in_=posture[:, c * HALF : (c + 1) * HALF].rearrange("(p t) j -> p t j", t=PACK),
-            )
-
-        load_posture(0)
         w3_raw[1, 0] = load_rows("w3_raw10", w3, 1, 0, PASS)
-        load_posture(1)
-        nc.sync.dma_start(out=gain_sb[:], in_=gain.rearrange("(g p t) -> p g t", p=P, t=PACK))
-        nc.sync.dma_start(out=skip_sb[:], in_=skip.rearrange("(g p t) -> p g t", p=P, t=PACK))
+        posture_sb = sb("posture_sb", [P, PACK, J], F32)
+        nc.sync.dma_start(out=posture_sb[:], in_=posture.rearrange("(p t) j -> p t j", t=PACK))
         w3_raw[0, 1] = load_rows("w3_raw01", w3, 0, PASS, N)
         w3_raw[1, 1] = load_rows("w3_raw11", w3, 1, PASS, N)
 
-        def deal(copy, grouped, raw, m0, m1, raw_m0=0):
+        def deal(copy, grouped, raw, m0, m1, walk="p m j t"):
             copy(
-                grouped[:, :, m0:m1, :].rearrange("p t m j -> p m t j"),
-                raw[:].rearrange("p j (m t) -> p m t j", t=PACK)[:, m0 - raw_m0 : m1 - raw_m0],
+                grouped[:, :, m0:m1, :].rearrange("p t m j -> " + walk),
+                raw[:].rearrange("p j (m t) -> " + walk, t=PACK)[:, m0:m1],
             )
 
         def quantize(codes, scales, values):
             nc.vector.quantize_mx(out=codes.bitcast(FP8X4), scales=scales, in_=values)
 
         nss = sb("nss", [P, PACK], F32)
-        nc.vector.scalar_tensor_tensor(nss[:], slope_sb[:], -1.0, share_sb[:], ALU.mult, ALU.mult)
+        ss = sb("ss", [P, PACK], F32)
+        nc.gpsimd.tensor_tensor(ss[:], slope_sb[:], share_sb[:], ALU.mult)
+        nc.gpsimd.tensor_scalar(nss[:], ss[:], -1.0, 0.0, ALU.mult, ALU.add)
+
+        def gpsimd_round(out, in_):
+            nc.gpsimd.tensor_scalar(out, in_, 1.0, 0.0, ALU.mult, ALU.add)
 
         w2_sb = sb("w2_sb", [P, 2 * N], U8)
         w2s_sb = sb("w2s_sb", [P, N], U8)
@@ -152,90 +149,91 @@ def tile_list_posture_relief_features_kernel(
                 stop=(a == k_passes - 1),
             )
 
+        bank_order = [(t0 + t, c) for t0 in (0, 2) for c in range(2) for t in range(2)]
+        for a in (0, 2, 1):
+            deal(nc.scalar.copy, w1_bf[a], w1_raw[a], 0, P)
+            quantize(w1_codes[a][:], w1_scales[a][:], w1_bf[a][:].rearrange("p t m j -> p (t m j)"))
         for a in range(k_passes):
-            nc.vector.tensor_copy(v_sb[a][:], tab_sb[a][:].indirect(offs_sb[:]))
             if a < k_passes - 1:
-                deal(nc.scalar.copy, w1_bf[a], w1_raw[a], 0, P)
-                quantize(w1_codes[a][:], w1_scales[a][:], w1_bf[a][:].rearrange("p t m j -> p (t m j)"))
+                nc.vector.tensor_copy(v_sb[a][:], tab_sb[a][:].indirect(offs_sb[:]))
             else:
                 for c in range(2):
-                    m0 = c * 64
-                    deal(nc.vector.tensor_copy, w1_bf[a], w1_last[c], m0, m0 + 42, m0)
-                    deal(nc.scalar.copy, w1_bf[a], w1_last[c], m0 + 42, m0 + 64, m0)
-                    for t in range(PACK):
-                        cols = slice(t * P + m0, t * P + m0 + 64)
-                        quantize(
-                            w1_codes[a][:, cols], w1_scales[a][:, cols],
-                            w1_bf[a][:, t, m0 : m0 + 64, :].rearrange("p m j -> p (m j)"),
-                        )
-            for t in range(PACK):
-                for c in range(2):
-                    mm1(a, t, c)
+                    nc.vector.tensor_copy(
+                        v_sb[a][:, c * BANK : (c + 1) * BANK],
+                        tab_sb[a][:].indirect(offs_sb[:, c * BANK // 16 : (c + 1) * BANK // 16]),
+                    )
+            for t, c in bank_order:
+                mm1(a, t, c)
 
         h_sb = [sb(f"h{t}", [P, S], F32) for t in range(PACK)]
         tops = sb("tops", [P, PACK, 2], F32)
         bias = sb("bias", [P, PACK], F32)
-        for t in range(PACK):
-            for c in range(2):
-                nc.vector.tensor_scalar(
-                    h_sb[t][:, c * BANK : (c + 1) * BANK], banks[2 * t + c][:], 1.0, None,
-                    ALU.mult, ALU.max, accum_out=tops[:, t, c : c + 1],
-                )
-            nc.gpsimd.tensor_scalar(
-                bias[:, t : t + 1], tops[:, t, 0:1], tops[:, t, 1:2], nss[:, t : t + 1], ALU.max, ALU.mult
+        for t, c in bank_order:
+            nc.vector.tensor_scalar(
+                h_sb[t][:, c * BANK : (c + 1) * BANK], banks[2 * t + c][:], 1.0,
+                tops[:, t, 0:1] if c == 1 else None,
+                ALU.mult, ALU.max, accum_out=tops[:, t, c : c + 1],
             )
+            if c == 1:
+                nc.scalar.activation(
+                    out=bias[:, t : t + 1], in_=tops[:, t, 1:2], func=ACT.Copy, scale=nss[:, t : t + 1]
+                )
 
         th = {}
         sd = {}
+        a_sb = [sb(f"a{c}", [P, PACK, HALF], F32) for c in range(2)]
+        picked = sb("picked", [P, PACK + 1, HALF], F32)
+        c_sb = [picked[:, c : c + PACK, :] for c in range(2)]
+        f_bf = [sb(f"f_bf{c}", [P, HALF, PACK], BF16) for c in range(2)]
 
-        def stage2(c):
-            cols16 = slice(c * HALF // 16, (c + 1) * HALF // 16)
-            a_sb = sb(f"a{c}", [P, PACK, HALF], F32)
-            c_sb = sb(f"c{c}", [P, PACK, HALF], F32)
-            for t in range(PACK):
-                nc.scalar.activation(
-                    out=a_sb[:, t, :], in_=h_sb[t][:].indirect(pos1_sb[:, cols16]), func=ACT.Sigmoid,
-                    bias=bias[:, t : t + 1], scale=slope_sb[:, t : t + 1],
-                )
-                nc.vector.tensor_tensor(
-                    c_sb[:, t, :], h_sb[t][:].indirect(pos2_sb[:, cols16]),
-                    posture_sb[c][:, t, :], ALU.mult,
-                )
-            f_bf = sb(f"f_bf{c}", [P, HALF, PACK], BF16)
+        def look(c, t):
+            nc.scalar.activation(
+                out=a_sb[c][:, t, :], in_=h_sb[t][:].indirect(pos1_sb[:, c * HALF // 16 : (c + 1) * HALF // 16]),
+                func=ACT.Sigmoid, bias=bias[:, t : t + 1], scale=slope_sb[:, t : t + 1],
+            )
+
+        def pick(c, t):
             nc.vector.tensor_tensor(
-                f_bf[:].rearrange("p (x i) t -> p x t i", i=LINE),
-                a_sb[:].rearrange("p t (x i) -> p x t i", i=LINE),
-                c_sb[:].rearrange("p t (x i) -> p x t i", i=LINE),
+                c_sb[c][:, t, :], h_sb[t][:].indirect(pos2_sb[:, c * HALF // 16 : (c + 1) * HALF // 16]),
+                posture_sb[:, t, c * HALF : (c + 1) * HALF], ALU.mult,
+            )
+
+        def make_f(c):
+            nc.vector.tensor_tensor(
+                f_bf[c][:].rearrange("p (x i) t -> p x t i", i=LINE),
+                a_sb[c][:].rearrange("p t (x i) -> p x t i", i=LINE),
+                c_sb[c].rearrange("p t (x i) -> p x t i", i=LINE),
                 ALU.mult,
             )
+
+        def mm2(c):
             f_codes = sb(f"f_codes{c}", [P, HALF], U32)
             f_scales = sb(f"f_scales{c}", [P, HALF], U8)
-            quantize(f_codes[:], f_scales[:], f_bf[:].rearrange("p j t -> p (j t)"))
-            for g in range(n_groups):
-                for t in range(PACK):
-                    s = PACK * g + t
-                    nc.tensor.matmul_mx(
-                        out=banks[4 * c + s // 2][:, (s % 2) * HALF : (s % 2 + 1) * HALF],
-                        lhsT=w2_sb[:, 2 * s * P : 2 * (s + 1) * P].bitcast(FP4X4),
-                        lhsT_scale=w2s_sb[:, s * P : (s + 1) * P],
-                        rhs=f_codes[:].bitcast(FP8X4),
-                        rhs_scale=f_scales[:],
-                        start=True,
-                        stop=True,
-                    )
+            quantize(f_codes[:], f_scales[:], f_bf[c][:].rearrange("p j t -> p (j t)"))
+            for s in range(n_groups * PACK):
+                nc.tensor.matmul_mx(
+                    out=banks[4 * c + s // 2][:, (s % 2) * HALF : (s % 2 + 1) * HALF],
+                    lhsT=w2_sb[:, 2 * s * P : 2 * (s + 1) * P].bitcast(FP4X4),
+                    lhsT_scale=w2s_sb[:, s * P : (s + 1) * P],
+                    rhs=f_codes[:].bitcast(FP8X4),
+                    rhs_scale=f_scales[:],
+                    start=True,
+                    stop=True,
+                )
 
         def tanh_d(c):
             for g in range(n_groups):
-                th[c, g] = sb(f"th{c}{g}", [P, 2, HALF, 2], F32, ["w1_raw0", "w1_raw1", "w1_last0", "w1_last1"][2 * c + g])
+                th[c, g] = sb(f"th{c}{g}", [P, PACK, HALF], F32, ["w1_raw0", "w1_raw1", "w1_raw2", "posture_sb"][2 * c + g])
                 for u in range(2):
                     nc.scalar.activation(
-                        out=th[c, g][:, u], in_=banks[4 * c + 2 * g + u][:].rearrange("p (e j) -> p j e", e=2),
+                        out=th[c, g][:, 2 * u : 2 * u + 2, :].rearrange("p t j -> p (t j)"),
+                        in_=banks[4 * c + 2 * g + u][:],
                         func=ACT.Tanh,
                     )
 
         def skip_d(c):
             for g in range(n_groups):
-                sd[c, g] = sb(f"sd{c}{g}", [P, PACK, HALF], F32, ["w1_bf0", "w1_bf1", "w1_bf2", "posture0"][2 * c + g])
+                sd[c, g] = sb(f"sd{c}{g}", [P, PACK, HALF], F32, ["w1_bf0", "w1_bf1", "w1_bf2", "picked"][2 * c + g])
                 for t in range(PACK):
                     nc.scalar.activation(
                         out=sd[c, g][:, t, :],
@@ -246,10 +244,18 @@ def tile_list_posture_relief_features_kernel(
         w3_codes = {}
         w3_scales = {}
 
-        def prep_w3(g, o):
-            bf = sb(f"w3_bf{g}{o}", [P, PACK, P, PACK], BF16)
+        w3_bf = {}
+
+        def round_w3(g, o, gpsimd_half=None):
+            w3_bf[g, o] = sb(f"w3_bf{g}{o}", [P, PACK, P, PACK], BF16)
             for c in range(2):
-                deal(nc.scalar.copy, bf, w3_raw[g, o], c * 64, (c + 1) * 64)
+                if c == gpsimd_half:
+                    deal(gpsimd_round, w3_bf[g, o], w3_raw[g, o], c * 64, (c + 1) * 64, "p m t j")
+                else:
+                    deal(nc.scalar.copy, w3_bf[g, o], w3_raw[g, o], c * 64, (c + 1) * 64)
+
+        def quant_w3(g, o):
+            bf = w3_bf[g, o]
             w3_codes[g, o] = sb(f"w3_codes{g}{o}", [P, PASS], U32)
             w3_scales[g, o] = sb(f"w3_scales{g}{o}", [P, PASS], U8)
             quantize(w3_codes[g, o][:], w3_scales[g, o][:], bf[:].rearrange("p t m j -> p (t m j)"))
@@ -257,39 +263,42 @@ def tile_list_posture_relief_features_kernel(
         t_codes = {}
         t_scales = {}
 
-        def quant_t(c):
-            for g in range(n_groups):
-                t_bf = sb(f"t_bf{c}{g}", [P, HALF, PACK], BF16, f"w3_raw{g}0" if c == 1 else None)
-                nc.vector.tensor_tensor(
-                    t_bf[:].rearrange("p j (u e) -> p j u e", e=2),
-                    th[c, g][:].rearrange("p u j e -> p j u e"),
-                    gain_sb[:, g, :].rearrange("p (u e) -> p u e", e=2).unsqueeze(1).to_broadcast([P, HALF, 2, 2]),
-                    ALU.mult,
-                )
-                t_codes[c, g] = sb(f"t_codes{c}{g}", [P, HALF], U32)
-                t_scales[c, g] = sb(f"t_scales{c}{g}", [P, HALF], U8)
-                quantize(t_codes[c, g][:], t_scales[c, g][:], t_bf[:].rearrange("p j t -> p (j t)"))
+        t_bf = {}
+
+        def make_t(c, g):
+            t_bf[c, g] = sb(f"t_bf{c}{g}", [P, HALF, PACK], BF16, f"w3_raw{g}0" if c == 1 else None)
+            nc.vector.tensor_tensor(
+                t_bf[c, g][:].rearrange("p (x i) t -> p x t i", i=LINE),
+                th[c, g][:].rearrange("p t (x i) -> p x t i", i=LINE),
+                gain_sb[:, g, :].unsqueeze(1).unsqueeze(3).to_broadcast([P, HALF // LINE, PACK, LINE]),
+                ALU.mult,
+            )
+
+        def quant_t(c, g):
+            t_codes[c, g] = sb(f"t_codes{c}{g}", [P, HALF], U32)
+            t_scales[c, g] = sb(f"t_scales{c}{g}", [P, HALF], U8)
+            quantize(t_codes[c, g][:], t_scales[c, g][:], t_bf[c, g][:].rearrange("p j t -> p (j t)"))
 
         y_scales = sb("y_scales", [P, n_groups, J], U8)
 
         y_sb = {}
         y_bf = {}
 
-        def mm3(c, o):
-            for t in range(PACK):
-                for g in range(n_groups):
+        def mm3(c, g):
+            for o in range(n_groups):
+                for t in range(PACK):
                     nc.tensor.matmul_mx(
                         out=banks[4 * c + 2 * o + t // 2][:, (t % 2) * HALF : (t % 2 + 1) * HALF],
                         lhsT=w3_codes[g, o][:, t * P : (t + 1) * P].bitcast(FP8X4),
                         lhsT_scale=w3_scales[g, o][:, t * P : (t + 1) * P],
                         rhs=t_codes[c, g][:].bitcast(FP8X4),
                         rhs_scale=t_scales[c, g][:],
-                        start=(g == 0),
-                        stop=(g == n_groups - 1),
+                        start=(g == 0 and t % 2 == 0),
+                        stop=(g == n_groups - 1 and t % 2 == 1),
                     )
 
         def add_y(c, o):
-            y_sb[c, o] = sb(f"y{c}{o}", [P, PACK, HALF], F32, f"{'ac'[o]}{c}")
+            y_sb[c, o] = sb(f"y{c}{o}", [P, PACK, HALF], F32, [["a0", "a1"], ["w3_raw01", "w3_raw11"]][c][o])
             for u in range(2):
                 nc.vector.tensor_tensor(
                     y_sb[c, o][:, 2 * u : 2 * u + 2, :].rearrange("p t j -> p (t j)"),
@@ -319,20 +328,40 @@ def tile_list_posture_relief_features_kernel(
                 in_=y_codes[:].bitcast(I32),
             )
 
-        stage2(0)
-        stage2(1)
+        round_w3(0, 0, 1)
+        for t in range(PACK):
+            look(0, t)
+            pick(0, t)
+        for t in range(PACK):
+            look(1, t)
+        pick(1, PACK - 1)
+        make_f(0)
+        quant_w3(0, 0)
+        mm2(0)
+        for t in range(PACK - 1):
+            pick(1, t)
+        round_w3(1, 0, 0)
+        quant_w3(1, 0)
+        make_f(1)
+        mm2(1)
         tanh_d(0)
-        prep_w3(0, 0)
-        prep_w3(1, 0)
-        prep_w3(0, 1)
-        prep_w3(1, 1)
-        quant_t(0)
+        round_w3(0, 1)
+        round_w3(1, 1)
+        make_t(0, 0)
+        make_t(0, 1)
+        quant_t(0, 0)
+        quant_t(0, 1)
+        quant_w3(0, 1)
+        quant_w3(1, 1)
         tanh_d(1)
         skip_d(0)
-        quant_t(1)
-        skip_d(1)
         mm3(0, 0)
         mm3(0, 1)
+        make_t(1, 0)
+        make_t(1, 1)
+        quant_t(1, 0)
+        quant_t(1, 1)
+        skip_d(1)
         add_y(0, 0)
         add_y(0, 1)
         mm3(1, 0)

@@ -50,7 +50,7 @@ def tile_list_posture_relief_features_kernel(
         tabs_sb = sb("tabs", [P, T], U8)
         w2s_raw = sb("w2s_raw", [P, N], U8)
         w2_raw = sb("w2_raw", [P, 2 * N], U8)
-        nc.gpsimd.memset(tabs_sb[:].bitcast(I32), 0)
+        nc.vector.memset(tabs_sb[:].bitcast(I32), 0)
         nc.vector.memset(w2s_raw[:].bitcast(I32), 0)
         for q in range(4):
             nc.gpsimd.dma_start(
@@ -61,8 +61,6 @@ def tile_list_posture_relief_features_kernel(
         share_sb = sb("share_sb", [P, PACK], F32)
         gain_sb = sb("gain_sb", [P, n_groups, PACK], F32)
         skip_sb = sb("skip_sb", [P, n_groups, PACK], F32)
-        nc.gpsimd.dma_start(out=slope_sb[:], in_=slope.rearrange("(p t) -> p t", t=PACK))
-        nc.gpsimd.dma_start(out=share_sb[:], in_=share.rearrange("(p t) -> p t", t=PACK))
         nc.gpsimd.dma_start(out=gain_sb[:], in_=gain.rearrange("(g p t) -> p g t", p=P, t=PACK))
         nc.gpsimd.dma_start(out=skip_sb[:], in_=skip.rearrange("(g p t) -> p g t", p=P, t=PACK))
 
@@ -82,23 +80,29 @@ def tile_list_posture_relief_features_kernel(
         w1_raw = {0: load_rows("w1_raw0", w1, 0, 0, H)}
         load_tab(0)
         nc.sync.dma_start(offs_sb[:], offs)
+        nc.sync.dma_start(pos1_sb[:], pos1)
+        nc.sync.dma_start(pos2_sb[:], pos2)
+        nc.sync.dma_start(out=w2_raw[:].bitcast(I32), in_=w2_words[0].bitcast(I32))
+        nc.sync.dma_start(out=slope_sb[:], in_=slope.rearrange("(p t) -> p t", t=PACK))
+        nc.sync.dma_start(out=share_sb[:], in_=share.rearrange("(p t) -> p t", t=PACK))
+        w1_raw[1] = load_rows("w1_raw1", w1, 1, 0, H)
+        w1_raw[2] = load_rows("w1_raw2", w1, 2, 0, H)
         for q in range(4):
             nc.sync.dma_start(
                 out=w2s_raw[32 * q : 32 * q + 4, :].bitcast(I32),
                 in_=w2_scales[0, 4 * q : 4 * q + 4, :].bitcast(I32),
             )
         load_tab(1)
-        nc.sync.dma_start(pos1_sb[:], pos1)
-        nc.sync.dma_start(pos2_sb[:], pos2)
-        w1_raw[2] = load_rows("w1_raw2", w1, 2, 0, H)
-        w1_raw[1] = load_rows("w1_raw1", w1, 1, 0, H)
-        nc.sync.dma_start(out=w2_raw[:].bitcast(I32), in_=w2_words[0].bitcast(I32))
         load_tab(2)
         w3_raw = {}
         w3_raw[0, 0] = load_rows("w3_raw00", w3, 0, 0, PASS)
         w3_raw[1, 0] = load_rows("w3_raw10", w3, 1, 0, PASS)
-        posture_sb = sb("posture_sb", [P, PACK, J], F32)
-        nc.sync.dma_start(out=posture_sb[:], in_=posture.rearrange("(p t) j -> p t j", t=PACK))
+        posture_sb = [sb(f"posture{c}", [P, PACK, HALF], F32) for c in range(2)]
+        for c in range(2):
+            nc.sync.dma_start(
+                out=posture_sb[c][:],
+                in_=posture[:, c * HALF : (c + 1) * HALF].rearrange("(p t) j -> p t j", t=PACK),
+            )
         w3_raw[0, 1] = load_rows("w3_raw01", w3, 0, PASS, N)
         w3_raw[1, 1] = load_rows("w3_raw11", w3, 1, PASS, N)
 
@@ -119,22 +123,11 @@ def tile_list_posture_relief_features_kernel(
         def gpsimd_round(out, in_):
             nc.gpsimd.tensor_scalar(out, in_, 1.0, 0.0, ALU.mult, ALU.add)
 
-        w2_sb = sb("w2_sb", [P, 2 * N], U8)
-        w2s_sb = sb("w2s_sb", [P, N], U8)
-        nc.vector.tensor_copy(
-            w2_sb[:].rearrange("p (g t m e) -> p g t m e", g=n_groups, t=PACK, e=2),
-            w2_raw[:].rearrange("p (g m t e) -> p g t m e", g=n_groups, t=PACK, e=2),
-        )
-        nc.vector.tensor_copy(
-            w2s_sb[:].rearrange("p (g t m) -> p g t m", g=n_groups, t=PACK),
-            w2s_raw[:].rearrange("p (g m t) -> p g t m", g=n_groups, t=PACK),
-        )
-
         vs_sb = sb("vs_sb", [P, S], U8)
         nc.vector.tensor_copy(vs_sb[:], tabs_sb[:].indirect(offs_sb[:]))
 
         v_sb = [sb(f"v{a}", [P, S], U32) for a in range(k_passes)]
-        w1_bf = [sb(f"w1_bf{a}", [P, PACK, P, PACK], BF16) for a in range(k_passes)]
+        w1_bf = [sb(f"w1_bf{a}", [P, PACK, P, PACK], BF16, "tabs" if a == 2 else None) for a in range(k_passes)]
         w1_codes = [sb(f"w1_codes{a}", [P, H], U32) for a in range(k_passes)]
         w1_scales = [sb(f"w1_scales{a}", [P, H], U8) for a in range(k_passes)]
 
@@ -150,20 +143,28 @@ def tile_list_posture_relief_features_kernel(
             )
 
         bank_order = [(t0 + t, c) for t0 in (0, 2) for c in range(2) for t in range(2)]
-        for a in (0, 2, 1):
+        for a in range(k_passes):
             deal(nc.scalar.copy, w1_bf[a], w1_raw[a], 0, P)
             quantize(w1_codes[a][:], w1_scales[a][:], w1_bf[a][:].rearrange("p t m j -> p (t m j)"))
         for a in range(k_passes):
-            if a < k_passes - 1:
-                nc.vector.tensor_copy(v_sb[a][:], tab_sb[a][:].indirect(offs_sb[:]))
-            else:
-                for c in range(2):
-                    nc.vector.tensor_copy(
-                        v_sb[a][:, c * BANK : (c + 1) * BANK],
-                        tab_sb[a][:].indirect(offs_sb[:, c * BANK // 16 : (c + 1) * BANK // 16]),
-                    )
+            for c in range(2):
+                nc.vector.tensor_copy(
+                    v_sb[a][:, c * BANK : (c + 1) * BANK],
+                    tab_sb[a][:].indirect(offs_sb[:, c * BANK // 16 : (c + 1) * BANK // 16]),
+                )
             for t, c in bank_order:
                 mm1(a, t, c)
+
+        w2_sb = sb("w2_sb", [P, 2 * N], U8)
+        w2s_sb = sb("w2s_sb", [P, N], U8)
+        nc.vector.tensor_copy(
+            w2_sb[:].rearrange("p (g t m e) -> p g t m e", g=n_groups, t=PACK, e=2),
+            w2_raw[:].rearrange("p (g m t e) -> p g t m e", g=n_groups, t=PACK, e=2),
+        )
+        nc.vector.tensor_copy(
+            w2s_sb[:].rearrange("p (g t m) -> p g t m", g=n_groups, t=PACK),
+            w2s_raw[:].rearrange("p (g m t) -> p g t m", g=n_groups, t=PACK),
+        )
 
         h_sb = [sb(f"h{t}", [P, S], F32) for t in range(PACK)]
         tops = sb("tops", [P, PACK, 2], F32)
@@ -195,7 +196,7 @@ def tile_list_posture_relief_features_kernel(
         def pick(c, t):
             nc.vector.tensor_tensor(
                 c_sb[c][:, t, :], h_sb[t][:].indirect(pos2_sb[:, c * HALF // 16 : (c + 1) * HALF // 16]),
-                posture_sb[:, t, c * HALF : (c + 1) * HALF], ALU.mult,
+                posture_sb[c][:, t, :], ALU.mult,
             )
 
         def make_f(c):
@@ -221,9 +222,9 @@ def tile_list_posture_relief_features_kernel(
                     stop=True,
                 )
 
-        def tanh_d(c):
-            for g in range(n_groups):
-                th[c, g] = sb(f"th{c}{g}", [P, PACK, HALF], F32, ["w1_raw0", "w1_raw1", "w1_raw2", "posture_sb"][2 * c + g])
+        def tanh_d(c, gs=(0, 1)):
+            for g in gs:
+                th[c, g] = sb(f"th{c}{g}", [P, PACK, HALF], F32, ["w1_raw0", "w1_raw1", "w1_raw2", "posture0"][2 * c + g])
                 for u in range(2):
                     nc.scalar.activation(
                         out=th[c, g][:, 2 * u : 2 * u + 2, :].rearrange("p t j -> p (t j)"),
@@ -231,9 +232,9 @@ def tile_list_posture_relief_features_kernel(
                         func=ACT.Tanh,
                     )
 
-        def skip_d(c):
-            for g in range(n_groups):
-                sd[c, g] = sb(f"sd{c}{g}", [P, PACK, HALF], F32, ["w1_bf0", "w1_bf1", "w1_bf2", "picked"][2 * c + g])
+        def skip_d(c, gs=(0, 1)):
+            for g in gs:
+                sd[c, g] = sb(f"sd{c}{g}", [P, PACK, HALF], F32, ["w1_bf0", "w1_bf1", "tabs", "picked"][2 * c + g])
                 for t in range(PACK):
                     nc.scalar.activation(
                         out=sd[c, g][:, t, :],
@@ -246,19 +247,19 @@ def tile_list_posture_relief_features_kernel(
 
         w3_bf = {}
 
-        def round_w3(g, o, gpsimd_half=None):
-            w3_bf[g, o] = sb(f"w3_bf{g}{o}", [P, PACK, P, PACK], BF16)
-            for c in range(2):
-                if c == gpsimd_half:
-                    deal(gpsimd_round, w3_bf[g, o], w3_raw[g, o], c * 64, (c + 1) * 64, "p m t j")
-                else:
-                    deal(nc.scalar.copy, w3_bf[g, o], w3_raw[g, o], c * 64, (c + 1) * 64)
+        def round_w3(g, o, u, copy, walk="p m j e", over=None):
+            w3_bf[g, o, u] = sb(f"w3_bf{g}{o}{u}", [P, 2, P, PACK], BF16, over)
+            copy(
+                w3_bf[g, o, u][:].rearrange("p e m j -> " + walk),
+                w3_raw[g, o][:].rearrange("p j (m u e) -> p u m j e", u=2, e=2)[:, u].rearrange("p m j e -> " + walk),
+            )
 
-        def quant_w3(g, o):
-            bf = w3_bf[g, o]
-            w3_codes[g, o] = sb(f"w3_codes{g}{o}", [P, PASS], U32)
-            w3_scales[g, o] = sb(f"w3_scales{g}{o}", [P, PASS], U8)
-            quantize(w3_codes[g, o][:], w3_scales[g, o][:], bf[:].rearrange("p t m j -> p (t m j)"))
+        def quant_w3(g, o, u):
+            w3_codes[g, o, u] = sb(f"w3_codes{g}{o}{u}", [P, 2 * P], U32)
+            w3_scales[g, o, u] = sb(f"w3_scales{g}{o}{u}", [P, 2 * P], U8)
+            quantize(
+                w3_codes[g, o, u][:], w3_scales[g, o, u][:], w3_bf[g, o, u][:].rearrange("p e m j -> p (e m j)")
+            )
 
         t_codes = {}
         t_scales = {}
@@ -284,17 +285,17 @@ def tile_list_posture_relief_features_kernel(
         y_sb = {}
         y_bf = {}
 
-        def mm3(c, g):
-            for o in range(n_groups):
-                for t in range(PACK):
+        def mm3(c, o):
+            for t in range(PACK):
+                for g in range(n_groups):
                     nc.tensor.matmul_mx(
                         out=banks[4 * c + 2 * o + t // 2][:, (t % 2) * HALF : (t % 2 + 1) * HALF],
-                        lhsT=w3_codes[g, o][:, t * P : (t + 1) * P].bitcast(FP8X4),
-                        lhsT_scale=w3_scales[g, o][:, t * P : (t + 1) * P],
+                        lhsT=w3_codes[g, o, t // 2][:, (t % 2) * P : (t % 2 + 1) * P].bitcast(FP8X4),
+                        lhsT_scale=w3_scales[g, o, t // 2][:, (t % 2) * P : (t % 2 + 1) * P],
                         rhs=t_codes[c, g][:].bitcast(FP8X4),
                         rhs_scale=t_scales[c, g][:],
-                        start=(g == 0 and t % 2 == 0),
-                        stop=(g == n_groups - 1 and t % 2 == 1),
+                        start=(g == 0),
+                        stop=(g == n_groups - 1),
                     )
 
         def add_y(c, o):
@@ -311,24 +312,30 @@ def tile_list_posture_relief_features_kernel(
                 in_=y_sb[c, o][:],
             )
 
-        def round_y(c, o, copy):
-            y_bf[c, o] = sb(f"y_bf{c}{o}", [P, HALF, PACK], BF16, f"w3_bf{c}{o}")
+        def round_y(c, o, copy, pair=LINE):
+            y_bf[c, o] = sb(f"y_bf{c}{o}", [P, HALF, PACK], BF16, f"w3_bf{c}{o}0")
             copy(
-                y_bf[c, o][:].rearrange("p (x i) t -> p x t i", i=LINE),
-                y_sb[c, o][:].rearrange("p t (x i) -> p x t i", i=LINE),
+                y_bf[c, o][:].rearrange("p (x i) t -> p x t i", i=pair),
+                y_sb[c, o][:].rearrange("p t (x i) -> p x t i", i=pair),
             )
+
+        y_codes = [sb(f"y_codes{c}", [P, n_groups, HALF], U32) for c in range(2)]
 
         def planes_y(c, o):
-            y_codes = sb(f"y_codes{c}{o}", [P, HALF], U32)
             quantize(
-                y_codes[:], y_scales[:, o, c * HALF : (c + 1) * HALF], y_bf[c, o][:].rearrange("p j t -> p (j t)")
-            )
-            nc.sync.dma_start(
-                out=out_1[o].rearrange("p j t -> p (j t)")[:, PACK * c * HALF : PACK * (c + 1) * HALF].bitcast(I32),
-                in_=y_codes[:].bitcast(I32),
+                y_codes[c][:, o, :], y_scales[:, o, c * HALF : (c + 1) * HALF],
+                y_bf[c, o][:].rearrange("p j t -> p (j t)"),
             )
 
-        round_w3(0, 0, 1)
+        def store_words(c):
+            nc.sync.dma_start(
+                out=out_1.rearrange("g p j t -> p g (j t)")[:, :, PACK * c * HALF : PACK * (c + 1) * HALF].bitcast(I32),
+                in_=y_codes[c][:].bitcast(I32),
+            )
+
+        round_w3(0, 0, 0, nc.scalar.copy)
+        round_w3(0, 0, 1, gpsimd_round, "p m e j")
+        round_w3(1, 0, 0, gpsimd_round, "p m e j")
         for t in range(PACK):
             look(0, t)
             pick(0, t)
@@ -336,46 +343,54 @@ def tile_list_posture_relief_features_kernel(
             look(1, t)
         pick(1, PACK - 1)
         make_f(0)
-        quant_w3(0, 0)
+        quant_w3(0, 0, 0)
         mm2(0)
         for t in range(PACK - 1):
             pick(1, t)
-        round_w3(1, 0, 0)
-        quant_w3(1, 0)
+        round_w3(1, 0, 1, nc.scalar.copy, over="tops")
+        quant_w3(0, 0, 1)
         make_f(1)
+        quant_w3(1, 0, 0)
         mm2(1)
         tanh_d(0)
-        round_w3(0, 1)
-        round_w3(1, 1)
+        quant_w3(1, 0, 1)
+        round_w3(0, 1, 0, nc.scalar.copy)
+        round_w3(0, 1, 1, nc.scalar.copy)
+        round_w3(1, 1, 0, nc.scalar.copy)
+        round_w3(1, 1, 1, nc.vector.tensor_copy)
         make_t(0, 0)
         make_t(0, 1)
         quant_t(0, 0)
         quant_t(0, 1)
-        quant_w3(0, 1)
-        quant_w3(1, 1)
-        tanh_d(1)
-        skip_d(0)
+        skip_d(0, (0,))
         mm3(0, 0)
+        for g in range(n_groups):
+            for u in range(2):
+                quant_w3(g, 1, u)
+        tanh_d(1)
+        add_y(0, 0)
+        skip_d(0, (1,))
         mm3(0, 1)
         make_t(1, 0)
         make_t(1, 1)
         quant_t(1, 0)
         quant_t(1, 1)
         skip_d(1)
-        add_y(0, 0)
         add_y(0, 1)
         mm3(1, 0)
         mm3(1, 1)
+        add_y(1, 0)
+        add_y(1, 1)
         round_y(0, 0, nc.scalar.copy)
         round_y(0, 1, nc.scalar.copy)
-        add_y(1, 0)
-        planes_y(0, 0)
-        add_y(1, 1)
         round_y(1, 0, nc.scalar.copy)
-        planes_y(0, 1)
         round_y(1, 1, nc.vector.tensor_copy)
+        planes_y(0, 0)
+        planes_y(0, 1)
+        store_words(0)
         planes_y(1, 0)
         planes_y(1, 1)
+        store_words(1)
         for q in range(4):
             (nc.scalar, nc.sync)[q % 2].dma_start(
                 out=out_2[:, 4 * q : 4 * q + 4, :].rearrange("g r j -> r g j").bitcast(I32),

@@ -46,6 +46,10 @@ def tile_list_posture_relief_features_kernel(
         pos1_sb = lists.tile([P, J // 16], U16, name="pos1_sb")
         pos2_sb = lists.tile([P, J // 16], U16, name="pos2_sb")
 
+        warm = sb("warm", [P, 2, 8], F32)
+        nc.gpsimd.memset(warm[:, 0, :], 0.0)
+        nc.scalar.activation(out=warm[:, 1, 0:1], in_=warm[:, 0, 0:1], func=ACT.Sigmoid)
+
         tab_sb = [sb(f"tab{a}", [P, T], U32) for a in range(k_passes)]
         tabs_sb = sb("tabs", [P, T], U8)
         w2s_raw = sb("w2s_raw", [P, N], U8)

from contextlib import ExitStack

import concourse.mybir as mybir

K, T, S, J, H, N = 1536, 4096, 1024, 512, 512, 1024
FLOPS = 2 * (K * H * S + H * N * J + N * N * J)

F32 = mybir.dt.float32
BF16 = mybir.dt.bfloat16
I32 = mybir.dt.int32
U32 = mybir.dt.uint32
U16 = mybir.dt.uint16
U8 = mybir.dt.uint8
FP8X4 = mybir.dt.float8_e4m3fn_x4
FP4X4 = mybir.dt.float4_e2m1fn_x4
ALU = mybir.AluOpType
ACT = mybir.ActivationFunctionType

P = 128
PACK = 4
PASS = P * PACK
BANK = 512
HALF = J // 2
LINE = 2


def tile_list_posture_relief_features_kernel(
    tc, tab_words, tab_scales, offs, pos1, pos2, w1, slope, share, posture,
    w2_words, w2_scales, gain, w3, skip, out_0, out_1, out_2,
):
    nc = tc.nc
    k_passes = K // PASS
    n_groups = N // PASS

    with ExitStack() as ctx:
        lists = ctx.enter_context(tc.tile_pool(name="lists", bufs=1))
        keep = ctx.enter_context(tc.tile_pool(name="keep", bufs=1))
        psum = ctx.enter_context(tc.psum_pool(name="psum", bufs=1))

        def sb(name, shape, dtype, over=None):
            return keep.tile(shape, dtype, name=name, tag=over or name, align_bytes=64)

        banks = [psum.tile([P, BANK], F32, name=f"bank{b}") for b in range(8)]

        offs_sb = lists.tile([P, S // 16], U16, name="offs_sb")
        pos1_sb = lists.tile([P, J // 16], U16, name="pos1_sb")
        pos2_sb = lists.tile([P, J // 16], U16, name="pos2_sb")

        warm = sb("warm", [P, 2, 8], F32)
        nc.gpsimd.memset(warm[:, 0, :], 0.0)
        nc.scalar.activation(out=warm[:, 1, 0:1], in_=warm[:, 0, 0:1], func=ACT.Sigmoid)

        tab_sb = [sb(f"tab{a}", [P, T], U32) for a in range(k_passes)]
        tabs_sb = sb("tabs", [P, T], U8)
        w2s_raw = sb("w2s_raw", [P, N], U8)
        w2_raw = sb("w2_raw", [P, 2 * N], U8)
        nc.vector.memset(tabs_sb[:].bitcast(I32), 0)
        nc.vector.memset(w2s_raw[:].bitcast(I32), 0)
        for q in range(4):
            nc.gpsimd.dma_start(
                out=tabs_sb[32 * q : 32 * q + 4 * k_passes, :].bitcast(I32),
                in_=tab_scales[:, 4 * q : 4 * q + 4, :].bitcast(I32),
            )
        slope_sb = sb("slope_sb", [P, PACK], F32)
        share_sb = sb("share_sb", [P, PACK], F32)
        gain_sb = sb("gain_sb", [P, n_groups, PACK], F32)
        skip_sb = sb("skip_sb", [P, n_groups, PACK], F32)
        nc.gpsimd.dma_start(out=gain_sb[:], in_=gain.rearrange("(g p t) -> p g t", p=P, t=PACK))
        nc.gpsimd.dma_start(out=skip_sb[:], in_=skip.rearrange("(g p t) -> p g t", p=P, t=PACK))

        def load_tab(a):
            nc.sync.dma_start(
                out=tab_sb[a][:].bitcast(I32),
                in_=tab_words[a].rearrange("p t i -> p (t i)").bitcast(I32),
            )

        def load_rows(name, w, a, c0, c1):
            raw = sb(name, [P, PACK, c1 - c0], F32)
            nc.sync.dma_start(
                out=raw[:], in_=w[a * PASS : (a + 1) * PASS, c0:c1].rearrange("(p j) c -> p j c", j=PACK)
            )
            return raw

        w1_raw = {0: load_rows("w1_raw0", w1, 0, 0, H)}
        load_tab(0)
        nc.sync.dma_start(offs_sb[:], offs)
        nc.sync.dma_start(pos1_sb[:], pos1)
        nc.sync.dma_start(pos2_sb[:], pos2)
        nc.sync.dma_start(out=w2_raw[:].bitcast(I32), in_=w2_words[0].bitcast(I32))
        nc.sync.dma_start(out=slope_sb[:], in_=slope.rearrange("(p t) -> p t", t=PACK))
        nc.sync.dma_start(out=share_sb[:], in_=share.rearrange("(p t) -> p t", t=PACK))
        w1_raw[1] = load_rows("w1_raw1", w1, 1, 0, H)
        w1_raw[2] = load_rows("w1_raw2", w1, 2, 0, H)
        for q in range(4):
            nc.sync.dma_start(
                out=w2s_raw[32 * q : 32 * q + 4, :].bitcast(I32),
                in_=w2_scales[0, 4 * q : 4 * q + 4, :].bitcast(I32),
            )
        load_tab(1)
        load_tab(2)
        w3_raw = {}
        w3_raw[0, 0] = load_rows("w3_raw00", w3, 0, 0, PASS)
        w3_raw[1, 0] = load_rows("w3_raw10", w3, 1, 0, PASS)
        posture_sb = [sb(f"posture{c}", [P, PACK, HALF], F32) for c in range(2)]
        for c in range(2):
            nc.sync.dma_start(
                out=posture_sb[c][:],
                in_=posture[:, c * HALF : (c + 1) * HALF].rearrange("(p t) j -> p t j", t=PACK),
            )
        w3_raw[0, 1] = load_rows("w3_raw01", w3, 0, PASS, N)
        w3_raw[1, 1] = load_rows("w3_raw11", w3, 1, PASS, N)

        def deal(copy, grouped, raw, m0, m1, walk="p m j t"):
            copy(
                grouped[:, :, m0:m1, :].rearrange("p t m j -> " + walk),
                raw[:].rearrange("p j (m t) -> " + walk, t=PACK)[:, m0:m1],
            )

        def quantize(codes, scales, values):
            nc.vector.quantize_mx(out=codes.bitcast(FP8X4), scales=scales, in_=values)

        nss = sb("nss", [P, PACK], F32)
        ss = sb("ss", [P, PACK], F32)
        nc.gpsimd.tensor_tensor(ss[:], slope_sb[:], share_sb[:], ALU.mult)
        nc.gpsimd.tensor_scalar(nss[:], ss[:], -1.0, 0.0, ALU.mult, ALU.add)

        def gpsimd_round(out, in_):
            nc.gpsimd.tensor_scalar(out, in_, 1.0, 0.0, ALU.mult, ALU.add)

        vs_sb = sb("vs_sb", [P, S], U8)
        nc.vector.tensor_copy(vs_sb[:], tabs_sb[:].indirect(offs_sb[:]))

        v_sb = [sb(f"v{a}", [P, S], U32) for a in range(k_passes)]
        w1_bf = [sb(f"w1_bf{a}", [P, PACK, P, PACK], BF16, "tabs" if a == 2 else None) for a in range(k_passes)]
        w1_codes = [sb(f"w1_codes{a}", [P, H], U32) for a in range(k_passes)]
        w1_scales = [sb(f"w1_scales{a}", [P, H], U8) for a in range(k_passes)]

        def mm1(a, t, c):
            nc.tensor.matmul_mx(
                out=banks[2 * t + c][:],
                lhsT=w1_codes[a][:, t * P : (t + 1) * P].bitcast(FP8X4),
                lhsT_scale=w1_scales[a][:, t * P : (t + 1) * P],
                rhs=v_sb[a][:, c * BANK : (c + 1) * BANK].bitcast(FP8X4),
                rhs_scale=vs_sb[4 * a : P, c * BANK : (c + 1) * BANK],
                start=(a == 0),
                stop=(a == k_passes - 1),
            )

        bank_order = [(t0 + t, c) for t0 in (0, 2) for c in range(2) for t in range(2)]
        for a in range(k_passes):
            deal(nc.scalar.copy, w1_bf[a], w1_raw[a], 0, P)
            quantize(w1_codes[a][:], w1_scales[a][:], w1_bf[a][:].rearrange("p t m j -> p (t m j)"))
        for a in range(k_passes):
            for c in range(2):
                nc.vector.tensor_copy(
                    v_sb[a][:, c * BANK : (c + 1) * BANK],
                    tab_sb[a][:].indirect(offs_sb[:, c * BANK // 16 : (c + 1) * BANK // 16]),
                )
            for t, c in bank_order:
                mm1(a, t, c)

        w2_sb = sb("w2_sb", [P, 2 * N], U8)
        w2s_sb = sb("w2s_sb", [P, N], U8)
        nc.vector.tensor_copy(
            w2_sb[:].rearrange("p (g t m e) -> p g t m e", g=n_groups, t=PACK, e=2),
            w2_raw[:].rearrange("p (g m t e) -> p g t m e", g=n_groups, t=PACK, e=2),
        )
        nc.vector.tensor_copy(
            w2s_sb[:].rearrange("p (g t m) -> p g t m", g=n_groups, t=PACK),
            w2s_raw[:].rearrange("p (g m t) -> p g t m", g=n_groups, t=PACK),
        )

        h_sb = [sb(f"h{t}", [P, S], F32) for t in range(PACK)]
        tops = sb("tops", [P, PACK, 2], F32)
        bias = sb("bias", [P, PACK], F32)
        for t, c in bank_order:
            nc.vector.tensor_scalar(
                h_sb[t][:, c * BANK : (c + 1) * BANK], banks[2 * t + c][:], 1.0,
                tops[:, t, 0:1] if c == 1 else None,
                ALU.mult, ALU.max, accum_out=tops[:, t, c : c + 1],
            )
            if c == 1:
                nc.scalar.activation(
                    out=bias[:, t : t + 1], in_=tops[:, t, 1:2], func=ACT.Copy, scale=nss[:, t : t + 1]
                )

        th = {}
        sd = {}
        a_sb = [sb(f"a{c}", [P, PACK, HALF], F32) for c in range(2)]
        picked = sb("picked", [P, PACK + 1, HALF], F32)
        c_sb = [picked[:, c : c + PACK, :] for c in range(2)]
        f_bf = [sb(f"f_bf{c}", [P, HALF, PACK], BF16) for c in range(2)]

        def look(c, t):
            nc.scalar.activation(
                out=a_sb[c][:, t, :], in_=h_sb[t][:].indirect(pos1_sb[:, c * HALF // 16 : (c + 1) * HALF // 16]),
                func=ACT.Sigmoid, bias=bias[:, t : t + 1], scale=slope_sb[:, t : t + 1],
            )

        def pick(c, t):
            nc.vector.tensor_tensor(
                c_sb[c][:, t, :], h_sb[t][:].indirect(pos2_sb[:, c * HALF // 16 : (c + 1) * HALF // 16]),
                posture_sb[c][:, t, :], ALU.mult,
            )

        def make_f(c):
            nc.vector.tensor_tensor(
                f_bf[c][:].rearrange("p (x i) t -> p x t i", i=LINE),
                a_sb[c][:].rearrange("p t (x i) -> p x t i", i=LINE),
                c_sb[c].rearrange("p t (x i) -> p x t i", i=LINE),
                ALU.mult,
            )

        def mm2(c):
            f_codes = sb(f"f_codes{c}", [P, HALF], U32)
            f_scales = sb(f"f_scales{c}", [P, HALF], U8)
            quantize(f_codes[:], f_scales[:], f_bf[c][:].rearrange("p j t -> p (j t)"))
            for s in range(n_groups * PACK):
                nc.tensor.matmul_mx(
                    out=banks[4 * c + s // 2][:, (s % 2) * HALF : (s % 2 + 1) * HALF],
                    lhsT=w2_sb[:, 2 * s * P : 2 * (s + 1) * P].bitcast(FP4X4),
                    lhsT_scale=w2s_sb[:, s * P : (s + 1) * P],
                    rhs=f_codes[:].bitcast(FP8X4),
                    rhs_scale=f_scales[:],
                    start=True,
                    stop=True,
                )

        def tanh_d(c, gs=(0, 1)):
            for g in gs:
                th[c, g] = sb(f"th{c}{g}", [P, PACK, HALF], F32, ["w1_raw0", "w1_raw1", "w1_raw2", "posture0"][2 * c + g])
                for u in range(2):
                    nc.scalar.activation(
                        out=th[c, g][:, 2 * u : 2 * u + 2, :].rearrange("p t j -> p (t j)"),
                        in_=banks[4 * c + 2 * g + u][:],
                        func=ACT.Tanh,
                    )

        def skip_d(c, gs=(0, 1)):
            for g in gs:
                sd[c, g] = sb(f"sd{c}{g}", [P, PACK, HALF], F32, ["w1_bf0", "w1_bf1", "tabs", "picked"][2 * c + g])
                for t in range(PACK):
                    nc.scalar.activation(
                        out=sd[c, g][:, t, :],
                        in_=banks[4 * c + 2 * g + t // 2][:, (t % 2) * HALF : (t % 2 + 1) * HALF],
                        func=ACT.Copy, scale=skip_sb[:, g, t : t + 1],
                    )

        w3_codes = {}
        w3_scales = {}

        w3_bf = {}

        def round_w3(g, o, u, copy, walk="p m j e", over=None):
            w3_bf[g, o, u] = sb(f"w3_bf{g}{o}{u}", [P, 2, P, PACK], BF16, over)
            copy(
                w3_bf[g, o, u][:].rearrange("p e m j -> " + walk),
                w3_raw[g, o][:].rearrange("p j (m u e) -> p u m j e", u=2, e=2)[:, u].rearrange("p m j e -> " + walk),
            )

        def quant_w3(g, o, u):
            w3_codes[g, o, u] = sb(f"w3_codes{g}{o}{u}", [P, 2 * P], U32)
            w3_scales[g, o, u] = sb(f"w3_scales{g}{o}{u}", [P, 2 * P], U8)
            quantize(
                w3_codes[g, o, u][:], w3_scales[g, o, u][:], w3_bf[g, o, u][:].rearrange("p e m j -> p (e m j)")
            )

        t_codes = {}
        t_scales = {}

        t_bf = {}

        def make_t(c, g):
            t_bf[c, g] = sb(f"t_bf{c}{g}", [P, HALF, PACK], BF16, f"w3_raw{g}0" if c == 1 else None)
            nc.vector.tensor_tensor(
                t_bf[c, g][:].rearrange("p (x i) t -> p x t i", i=LINE),
                th[c, g][:].rearrange("p t (x i) -> p x t i", i=LINE),
                gain_sb[:, g, :].unsqueeze(1).unsqueeze(3).to_broadcast([P, HALF // LINE, PACK, LINE]),
                ALU.mult,
            )

        def quant_t(c, g):
            t_codes[c, g] = sb(f"t_codes{c}{g}", [P, HALF], U32)
            t_scales[c, g] = sb(f"t_scales{c}{g}", [P, HALF], U8)
            quantize(t_codes[c, g][:], t_scales[c, g][:], t_bf[c, g][:].rearrange("p j t -> p (j t)"))

        y_scales = sb("y_scales", [P, n_groups, J], U8)

        y_sb = {}
        y_bf = {}

        def mm3(c, o):
            for t in range(PACK):
                for g in range(n_groups):
                    nc.tensor.matmul_mx(
                        out=banks[4 * c + 2 * o + t // 2][:, (t % 2) * HALF : (t % 2 + 1) * HALF],
                        lhsT=w3_codes[g, o, t // 2][:, (t % 2) * P : (t % 2 + 1) * P].bitcast(FP8X4),
                        lhsT_scale=w3_scales[g, o, t // 2][:, (t % 2) * P : (t % 2 + 1) * P],
                        rhs=t_codes[c, g][:].bitcast(FP8X4),
                        rhs_scale=t_scales[c, g][:],
                        start=(g == 0),
                        stop=(g == n_groups - 1),
                    )

        def add_y(c, o):
            y_sb[c, o] = sb(f"y{c}{o}", [P, PACK, HALF], F32, [["a0", "a1"], ["w3_raw01", "w3_raw11"]][c][o])
            for u in range(2):
                nc.vector.tensor_tensor(
                    y_sb[c, o][:, 2 * u : 2 * u + 2, :].rearrange("p t j -> p (t j)"),
                    banks[4 * c + 2 * o + u][:],
                    sd[c, o][:, 2 * u : 2 * u + 2, :].rearrange("p t j -> p (t j)"),
                    ALU.add,
                )
            nc.sync.dma_start(
                out=out_0[o * PASS : (o + 1) * PASS, c * HALF : (c + 1) * HALF].rearrange("(p t) j -> p t j", t=PACK),
                in_=y_sb[c, o][:],
            )

        def round_y(c, o, copy, pair=LINE):
            y_bf[c, o] = sb(f"y_bf{c}{o}", [P, HALF, PACK], BF16, f"w3_bf{c}{o}0")
            copy(
                y_bf[c, o][:].rearrange("p (x i) t -> p x t i", i=pair),
                y_sb[c, o][:].rearrange("p t (x i) -> p x t i", i=pair),
            )

        y_codes = [sb(f"y_codes{c}", [P, n_groups, HALF], U32) for c in range(2)]

        def planes_y(c, o):
            quantize(
                y_codes[c][:, o, :], y_scales[:, o, c * HALF : (c + 1) * HALF],
                y_bf[c, o][:].rearrange("p j t -> p (j t)"),
            )

        def store_words(c):
            nc.sync.dma_start(
                out=out_1.rearrange("g p j t -> p g (j t)")[:, :, PACK * c * HALF : PACK * (c + 1) * HALF].bitcast(I32),
                in_=y_codes[c][:].bitcast(I32),
            )

        round_w3(0, 0, 0, nc.scalar.copy)
        round_w3(0, 0, 1, gpsimd_round, "p m e j")
        round_w3(1, 0, 0, gpsimd_round, "p m e j")
        for t in range(PACK):
            look(0, t)
            pick(0, t)
        for t in range(PACK):
            look(1, t)
        pick(1, PACK - 1)
        make_f(0)
        quant_w3(0, 0, 0)
        mm2(0)
        for t in range(PACK - 1):
            pick(1, t)
        round_w3(1, 0, 1, nc.scalar.copy, over="tops")
        quant_w3(0, 0, 1)
        make_f(1)
        quant_w3(1, 0, 0)
        mm2(1)
        tanh_d(0)
        quant_w3(1, 0, 1)
        round_w3(0, 1, 0, nc.scalar.copy)
        round_w3(0, 1, 1, nc.scalar.copy)
        round_w3(1, 1, 0, nc.scalar.copy)
        round_w3(1, 1, 1, nc.vector.tensor_copy)
        make_t(0, 0)
        make_t(0, 1)
        quant_t(0, 0)
        quant_t(0, 1)
        skip_d(0, (0,))
        mm3(0, 0)
        for g in range(n_groups):
            for u in range(2):
                quant_w3(g, 1, u)
        tanh_d(1)
        add_y(0, 0)
        skip_d(0, (1,))
        mm3(0, 1)
        make_t(1, 0)
        make_t(1, 1)
        quant_t(1, 0)
        quant_t(1, 1)
        skip_d(1)
        add_y(0, 1)
        mm3(1, 0)
        mm3(1, 1)
        add_y(1, 0)
        add_y(1, 1)
        round_y(0, 0, nc.scalar.copy)
        round_y(0, 1, nc.scalar.copy)
        round_y(1, 0, nc.scalar.copy)
        round_y(1, 1, nc.vector.tensor_copy)
        planes_y(0, 0)
        planes_y(0, 1)
        store_words(0)
        planes_y(1, 0)
        planes_y(1, 1)
        store_words(1)
        for q in range(4):
            (nc.scalar, nc.sync)[q % 2].dma_start(
                out=out_2[:, 4 * q : 4 * q + 4, :].rearrange("g r j -> r g j").bitcast(I32),
                in_=y_scales[32 * q : 32 * q + 4].bitcast(I32),
            )
